import numpy as np
import ml_dtypes


def mxq(x, axis, fmt="e4m3"):
    dtype, down = {"e4m3": (ml_dtypes.float8_e4m3fn, 7), "e5m2": (ml_dtypes.float8_e5m2, 14)}[fmt]
    v = np.moveaxis(np.asarray(x, np.float32).astype(ml_dtypes.bfloat16).astype(np.float64), axis, -1)
    blocks = v.reshape(v.shape[:-1] + (-1, 32))
    amax = np.abs(blocks).max(-1, keepdims=True)
    byte = np.maximum(np.where(amax > 0, np.frexp(amax)[1] - 1 + 127, 0) - down, 1)
    scale = np.exp2(byte - 127.0)
    codes = (blocks / scale).astype(np.float32).astype(dtype).astype(np.float64)
    return np.moveaxis((codes * scale).reshape(v.shape), -1, axis)


WIDE = False


def mx_kscale(k):
    if not WIDE:
        return np.ones(k)
    levels = np.array([10, -10, 5, -5, 0])
    if k % 512:
        return np.exp2(np.random.permutation(np.resize(levels, k // 32))).repeat(32)
    a = np.empty((k // 512, 16))
    for p in range(k // 512):
        a[p, :8] = np.random.permutation(np.resize(levels, 8))
        for g in range(8):
            far = levels[np.abs(levels - a[p, g]) >= 10]
            a[p, g + 8] = far[np.random.randint(len(far))]
    return np.exp2(a.ravel()).repeat(32)


def f64(x):
    return np.asarray(x).astype(np.float64)


def striped(idx):
    return np.tile(idx.reshape(-1, 16).T, (8, 1)).astype(np.uint16)


def unstriped(offs):
    return offs[:16].T.reshape(-1).astype(np.int64)


def striped8(idx):
    return np.concatenate([x.reshape(-1, 16).T for x in idx]).astype(np.uint16)


def runs(offs, k):
    lists = np.stack([offs[16 * r : 16 * r + 16].T.reshape(-1) for r in range(8)]).astype(np.int64)
    return lists[np.arange(k) % 512 // 64]


def pack_weight(w):
    k, n = w.shape
    w = f64(np.asarray(w, np.float32).astype(ml_dtypes.bfloat16)).reshape(k // 32, 32, n)
    amax = np.abs(w).max(1)
    byte = np.clip(np.where(amax > 0, np.frexp(amax)[1] - 1 + 127 - 7, 1), 1, 254)
    scaled = (w * np.exp2(127.0 - byte)[:, None, :]).reshape(k, n).astype(np.float32)
    words = np.ascontiguousarray(scaled.reshape(k // 512, 128, 4, n).transpose(0, 1, 3, 2)).astype(ml_dtypes.float8_e4m3fn).view(np.uint8)
    return words, np.ascontiguousarray(byte.astype(np.uint8).reshape(k // 512, 16, n))


def unpack_weight(words, scales):
    g, p, n, _ = words.shape
    vals = np.ascontiguousarray(words).view(ml_dtypes.float8_e4m3fn).astype(np.float64) * np.repeat(np.exp2(scales.astype(np.float64) - 127.0), 8, axis=1)[..., None]
    return vals.transpose(0, 1, 3, 2).reshape(g * 512, n)


def sigmoid(v):
    return 1.0 / (1.0 + np.exp(-np.maximum(v, -700.0)))

def planes(y):
    n, m = y.shape
    v = y.astype(np.float32).astype(ml_dtypes.bfloat16).astype(np.float64).reshape(n // 32, 32, m)
    top = np.abs(v).max(1)
    byte = np.clip(np.where(top > 0, np.frexp(top)[1] - 1 + 127 - 7, 1), 1, 254)
    codes = (v * np.exp2(127.0 - byte)[:, None, :]).reshape(n, m).astype(np.float32).astype(ml_dtypes.float8_e4m3fn).view(np.uint8)
    words = codes.reshape(n // 512, 128, 4, m).transpose(0, 1, 3, 2)
    return np.ascontiguousarray(words), np.ascontiguousarray(byte.astype(np.uint8).reshape(n // 512, 16, m))


K, T, S, G, H, W, U = 512, 2048, 512, 2048, 512, 1024, 256


def setup_inputs():
    n = np.random.standard_normal
    s = mx_kscale(K)[:, None]
    u = mx_kscale(S)
    packed_xT = pack_weight(n((K, T)) * s)
    packed_dT = pack_weight(n((K, G)) / s)
    perm = np.random.permutation(S)
    return {
        "x_words": packed_xT[0],
        "x_scales": packed_xT[1],
        "d_words": packed_dT[0],
        "d_scales": packed_dT[1],
        "ga": (np.random.uniform(0.5, 1.5, (H, 1)) * u[:, None]).astype(np.float32),
        "gb": (np.random.uniform(0.5, 1.5, (H, 1)) / u[:, None]).astype(np.float32),
        "offs": striped(np.random.permutation(T)[:S]),
        "kidx": striped8(np.random.randint(0, G, (8, H))),
        "n1": striped(np.random.randint(0, S, W)),
        "n2": striped8(np.stack([np.random.permutation(S) for _ in range(8)])),
        "n3": striped8(np.stack([np.random.permutation(S) for _ in range(8)])),
        "n4": striped(perm[:U]),
        "n5": striped(perm[U:]),
    }


def reference(x_words, x_scales, d_words, d_scales, ga, gb, offs, kidx, n1, n2, n3, n4, n5):
    d_kidx = unpack_weight(d_words, d_scales)[np.arange(K)[:, None], runs(kidx, K)]
    xq = unpack_weight(x_words, x_scales)[:, unstriped(offs)]
    s = 0.0625 * (d_kidx.T @ xq)
    mb = s[:, unstriped(n1)]
    ms = mb.reshape(H, S, 2).sum(axis=2)
    mx = mb.reshape(H, S, 2).max(axis=2)
    z = f64(ga) * (ms - np.maximum(s, mx))
    z2 = f64(gb) * (s * (s[np.arange(H)[:, None], runs(n2, H)] - (s[np.arange(H)[:, None], runs(n3, H)])))
    cm = 0.0625 * ((mxq(z, 0, "e4m3").T @ mxq(z2, 0, "e4m3")))
    pa = cm[:, unstriped(n4)]
    pb = cm[:, unstriped(n5)]
    ra = pa * sigmoid(pb)
    out = cm.copy()
    out[:, unstriped(n5)] = ra
    return (out,) + planes(out)

@@ -1,0 +1,289 @@
+from contextlib import ExitStack
+
+import concourse.mybir as mybir
+
+K, T, S, G, H, W, U = 512, 2048, 512, 2048, 512, 1024, 256
+FLOPS = 2 * K * H * S + 2 * H * S * S
+
+F32 = mybir.dt.float32
+BF16 = mybir.dt.bfloat16
+U32 = mybir.dt.uint32
+I32 = mybir.dt.int32
+U16 = mybir.dt.uint16
+U8 = mybir.dt.uint8
+FP8X4 = mybir.dt.float8_e4m3fn_x4
+ALU = mybir.AluOpType
+ACT = mybir.ActivationFunctionType
+
+P = 128
+PACK = 4
+HALF = S // 2
+SIXTEENTH = 0.0625
+
+
+def tile_picked_simkgpairwindfold_none_po_kernel(
+    tc, x_words, x_scales, d_words, d_scales, ga, gb, offs, kidx, n1, n2, n3, n4, n5, out_0, out_1, out_2
+):
+    nc = tc.nc
+    with ExitStack() as ctx:
+        keep = ctx.enter_context(tc.tile_pool(name="keep", bufs=1))
+        psum = ctx.enter_context(tc.psum_pool(name="psum", bufs=1))
+
+        def tile(shape, dtype, name):
+            return keep.tile(shape, dtype, name=name, align_bytes=64)
+
+        def load_list(src, name):
+            lst = keep.tile(list(src.shape), U16, name=name)
+            nc.sync.dma_start(lst[:], src)
+            return lst
+
+        def entries(lst, first, count):
+            return lst[:, first // 16 : (first + count) // 16]
+
+        d_bytes = tile([P, G], U8, "d_bytes")
+        x_bytes = tile([P, T], U8, "x_bytes")
+        nc.vector.memset(x_bytes[:].bitcast(I32), 0)
+        kidx_l = load_list(kidx, "kidx_l")
+        nc.sync.dma_start(
+            d_bytes[:].bitcast(I32),
+            d_scales[0].bitcast(I32).rearrange("q (a n) -> q a n", a=1).to_broadcast([16, 8, G // 4]),
+        )
+        d_tab = tile([P, G], U32, "d_tab")
+        nc.sync.dma_start(d_tab[:].bitcast(I32), d_words[0].rearrange("p n t -> p (n t)").bitcast(I32))
+        x_tab = tile([P, T], U32, "x_tab")
+        nc.sync.dma_start(x_tab[:].bitcast(I32), x_words[0].rearrange("p n t -> p (n t)").bitcast(I32))
+        offs_l = load_list(offs, "offs_l")
+        for q in range(4):
+            nc.scalar.dma_start(x_bytes[32 * q : 32 * q + 4, :].bitcast(I32), x_scales[0, 4 * q : 4 * q + 4, :].bitcast(I32))
+        n1_l = load_list(n1, "n1_l")
+        n3_l = load_list(n3, "n3_l")
+        n2_l = load_list(n2, "n2_l")
+        ga_t = tile([P, PACK], F32, "ga_t")
+        nc.sync.dma_start(ga_t[:], ga.rearrange("(p t) o -> p (t o)", t=PACK))
+        gb_t = tile([P, PACK], F32, "gb_t")
+        nc.sync.dma_start(gb_t[:], gb.rearrange("(p t) o -> p (t o)", t=PACK))
+        n5_l = load_list(n5, "n5_l")
+        n4_l = load_list(n4, "n4_l")
+
+        key_bytes = tile([P, H], U8, "key_bytes")
+        nc.vector.tensor_copy(key_bytes[:], d_bytes[:].indirect(kidx_l[:]))
+        key_bytes_dealt = tile([P, H], U8, "key_bytes_dealt")
+        nc.vector.tensor_copy(
+            key_bytes_dealt[:].rearrange("p (t m) -> p m t", t=PACK), key_bytes[:].rearrange("p (m t) -> p m t", t=PACK)
+        )
+        key_scale = tile([P, H], U8, "key_scale")
+        for i in range(4):
+            nc.scalar.dma_start(key_scale[i:P:32, :].bitcast(I32), key_bytes_dealt[8 * i : P : 32, :].bitcast(I32))
+        key_words = tile([P, H], U32, "key_words")
+        nc.vector.tensor_copy(key_words[:], d_tab[:].indirect(kidx_l[:]))
+        key_codes = tile([P, H], U32, "key_codes")
+        nc.vector.tensor_copy(
+            key_codes[:].bitcast(I32).rearrange("p (t m) -> p m t", t=PACK),
+            key_words[:].bitcast(I32).rearrange("p (m t) -> p m t", t=PACK),
+        )
+        tok_scale = tile([P, S], U8, "tok_scale")
+        nc.vector.tensor_copy(tok_scale[:], x_bytes[:].indirect(offs_l[:]))
+        tok_codes = tile([P, S], U32, "tok_codes")
+        nc.vector.tensor_copy(tok_codes[:], x_tab[:].indirect(offs_l[:]))
+
+        s_bank = [psum.tile([P, S], F32, name="s_bank%d" % t) for t in range(PACK)]
+        for t in range(PACK):
+            cols = slice(P * t, P * (t + 1))
+            nc.tensor.matmul_mx(
+                out=s_bank[t][:],
+                lhsT=key_codes[:, cols].bitcast(FP8X4),
+                lhsT_scale=key_scale[:, cols],
+                rhs=tok_codes[:].bitcast(FP8X4),
+                rhs_scale=tok_scale[:],
+                start=True,
+                stop=True,
+            )
+
+        s = [tile([P, S], F32, "s%d" % t) for t in range(PACK)]
+        mb = [tile([P, W], F32, "mb%d" % t) for t in range(PACK)]
+        low = tile([P, PACK, S], F32, "low")
+        z2 = [tile([P, PACK, HALF], F32, "z2_%d" % h) for h in range(2)]
+
+        def evac_s(t, on_vector):
+            if on_vector:
+                nc.vector.tensor_scalar(s[t][:], s_bank[t][:], SIXTEENTH, None, ALU.mult)
+            else:
+                nc.scalar.activation(s[t][:], s_bank[t][:], ACT.Copy, scale=SIXTEENTH)
+
+        def members(t):
+            for first, count in ((0, 352), (352, 352), (704, 320)):
+                nc.scalar.activation(mb[t][:, first : first + count], s[t][:].indirect(entries(n1_l, first, count)), ACT.Copy)
+
+        def fold(t):
+            a = mb[t][:, 0:W:2]
+            b = mb[t][:, 1:W:2]
+            e = tile([P, S], F32, "e%d" % t)
+            nc.vector.tensor_tensor(e[:], a, s[t][:], ALU.subtract)
+            f = tile([P, S], F32, "f%d" % t)
+            nc.vector.scalar_tensor_tensor(f[:], e[:], 0.0, b, ALU.min, ALU.add)
+            nc.vector.tensor_tensor(low[:, t, :], f[:], a, ALU.min)
+
+        def weigh(t, h, diff):
+            nc.vector.scalar_tensor_tensor(
+                z2[h][:, t, :], diff[:], gb_t[:, t : t + 1], s[t][:, HALF * h : HALF * (h + 1)], ALU.mult, ALU.mult
+            )
+
+        def diff_on_vector(t, h):
+            at3 = tile([P, HALF], F32, "at3_%d_%d" % (t, h))
+            nc.vector.tensor_copy(at3[:], s[t][:].indirect(entries(n3_l, HALF * h, HALF)))
+            diff = tile([P, HALF], F32, "diff_%d_%d" % (t, h))
+            nc.vector.tensor_tensor(diff[:], s[t][:].indirect(entries(n2_l, HALF * h, HALF)), at3[:], ALU.subtract)
+            weigh(t, h, diff)
+
+        def fetch_on_scalar(t, h):
+            at3 = tile([P, HALF], F32, "at3_%d_%d" % (t, h))
+            nc.scalar.activation(at3[:], s[t][:].indirect(entries(n3_l, HALF * h, HALF)), ACT.Copy)
+            at2 = tile([P, HALF], F32, "at2_%d_%d" % (t, h))
+            nc.scalar.activation(at2[:], s[t][:].indirect(entries(n2_l, HALF * h, HALF)), ACT.Copy)
+            return at2, at3
+
+        def diff_of(t, h, pair):
+            diff = tile([P, HALF], F32, "diff_%d_%d" % (t, h))
+            nc.vector.tensor_tensor(diff[:], pair[0][:], pair[1][:], ALU.subtract)
+            weigh(t, h, diff)
+
+        evac_s(0, False)
+        evac_s(1, True)
+        evac_s(2, False)
+        evac_s(3, True)
+        members(0)
+        diff_on_vector(0, 0)
+        diff_on_vector(1, 0)
+        members(1)
+        fold(0)
+        members(2)
+        fold(1)
+        members(3)
+        fold(2)
+        fold(3)
+        pairs0 = [fetch_on_scalar(t, 0) for t in (2, 3)]
+        pairs1 = [fetch_on_scalar(t, 1) for t in range(PACK)]
+
+        z_bf = tile([P, S * PACK], BF16, "z_bf")
+        nc.vector.tensor_tensor(
+            z_bf[:].rearrange("p (r m t) -> p m t r", r=PACK, t=PACK),
+            low[:].rearrange("p t (m r) -> p m t r", r=PACK),
+            ga_t[:].rearrange("p (a t b) -> p a t b", a=1, b=1).to_broadcast([P, P, PACK, PACK]),
+            ALU.mult,
+        )
+        z_codes = tile([P, S], U32, "z_codes")
+        z_scale = tile([P, S], U8, "z_scale")
+        nc.vector.quantize_mx(out=z_codes[:].bitcast(FP8X4), scales=z_scale[:], in_=z_bf[:])
+
+        cm_bank = [psum.tile([P, S], F32, name="cm_bank%d" % t) for t in range(PACK)]
+        res = [tile([P, S], F32, "res%d" % t) for t in range(PACK)]
+
+        def second_product(h):
+            cols = slice(HALF * h, HALF * (h + 1))
+            y_bf = tile([P, HALF * PACK], BF16, "y_bf%d" % h)
+            nc.vector.tensor_copy(
+                y_bf[:].rearrange("p (c i t) -> p c t i", i=4, t=PACK), z2[h][:].rearrange("p t (c i) -> p c t i", i=4)
+            )
+            y_codes = tile([P, HALF], U32, "y_codes%d" % h)
+            y_scale = tile([P, HALF], U8, "y_scale%d" % h)
+            nc.vector.quantize_mx(out=y_codes[:].bitcast(FP8X4), scales=y_scale[:], in_=y_bf[:])
+            for t in range(PACK):
+                rows = slice(P * t, P * (t + 1))
+                nc.tensor.matmul_mx(
+                    out=cm_bank[t][:, cols],
+                    lhsT=z_codes[:, rows].bitcast(FP8X4),
+                    lhsT_scale=z_scale[:, rows],
+                    rhs=y_codes[:].bitcast(FP8X4),
+                    rhs_scale=y_scale[:],
+                    start=True,
+                    stop=True,
+                )
+
+        def evac_cm(t, h, on_vector):
+            cols = slice(HALF * h, HALF * (h + 1))
+            if on_vector:
+                nc.vector.tensor_scalar(res[t][:, cols], cm_bank[t][:, cols], SIXTEENTH, None, ALU.mult)
+            else:
+                nc.scalar.activation(res[t][:, cols], cm_bank[t][:, cols], ACT.Copy, scale=SIXTEENTH)
+
+        diff_of(2, 0, pairs0[0])
+        diff_of(3, 0, pairs0[1])
+        second_product(0)
+        for t in range(PACK):
+            diff_of(t, 1, pairs1[t])
+        for t in range(PACK):
+            evac_cm(t, 0, False)
+        second_product(1)
+
+        gate = [tile([P, U], F32, "gate%d" % t) for t in range(PACK)]
+        part = [tile([P, U], F32, "part%d" % t) for t in range(PACK)]
+        rounded = tile([P, PACK, S], BF16, "rounded")
+        out_rows = out_0.rearrange("(p t) j -> p t j", t=PACK)
+
+        def sig(t):
+            nc.scalar.activation(gate[t][:], res[t][:].indirect(n5_l[:]), ACT.Sigmoid)
+
+        def fetch_a(t, on_vector):
+            if on_vector:
+                nc.vector.tensor_copy(part[t][:], res[t][:].indirect(n4_l[:]))
+            else:
+                nc.scalar.activation(part[t][:], res[t][:].indirect(n4_l[:]), ACT.Copy)
+
+        def fetch_mul(t):
+            nc.vector.tensor_tensor(part[t][:], res[t][:].indirect(n4_l[:]), gate[t][:], ALU.mult)
+
+        def put_mul(t):
+            nc.vector.tensor_tensor(res[t][:].indirect(n5_l[:]), part[t][:], gate[t][:], ALU.mult)
+
+        def put(t):
+            nc.scalar.activation(res[t][:].indirect(n5_l[:]), part[t][:], ACT.Copy)
+
+        def store(t):
+            nc.sync.dma_start(out_rows[:, t, :], res[t][:])
+
+        def rnd(t, on_vector):
+            if on_vector:
+                nc.vector.tensor_copy(rounded[:, t, :], res[t][:])
+            else:
+                nc.scalar.copy(rounded[:, t, :], res[t][:])
+
+        evac_cm(1, 1, True)
+        evac_cm(0, 1, False)
+        evac_cm(2, 1, True)
+        sig(1)
+        fetch_a(2, True)
+        sig(0)
+        fetch_mul(1)
+        fetch_a(0, False)
+        evac_cm(3, 1, False)
+        put_mul(0)
+        store(0)
+        sig(3)
+        sig(2)
+        put(1)
+        store(1)
+        fetch_mul(3)
+        put_mul(2)
+        store(2)
+        put(3)
+        store(3)
+        for t in (0, 1, 2, 3):
+            rnd(t, True)
+
+        woven = tile([P, S * PACK], BF16, "woven")
+        cut = 160
+        nc.scalar.copy(
+            woven[:, : cut * PACK].rearrange("p (c i t) -> p c t i", i=4, t=PACK),
+            rounded[:, :, :cut].rearrange("p t (c i) -> p c t i", i=4),
+        )
+        nc.vector.tensor_copy(
+            woven[:, cut * PACK :].rearrange("p (c i t) -> p c t i", i=4, t=PACK),
+            rounded[:, :, cut:].rearrange("p t (c i) -> p c t i", i=4),
+        )
+        out_codes = tile([P, S], U32, "out_codes")
+        out_scale = tile([P, S], U8, "out_scale")
+        nc.vector.quantize_mx(out=out_codes[:].bitcast(FP8X4), scales=out_scale[:], in_=woven[:])
+        nc.sync.dma_start(out_1[0].rearrange("p n t -> p (n t)").bitcast(I32), out_codes[:].bitcast(I32))
+        for q in range(4):
+            queue = nc.scalar if q % 2 == 0 else nc.sync
+            queue.dma_start(out_2[0, 4 * q : 4 * q + 4, :].bitcast(I32), out_scale[32 * q : 32 * q + 4, :].bitcast(I32))

@@ -42,26 +42,32 @@ def tile_picked_simkgpairwindfold_none_po_kernel(
 
         d_bytes = tile([P, G], U8, "d_bytes")
         x_bytes = tile([P, T], U8, "x_bytes")
-        nc.vector.memset(x_bytes[:].bitcast(I32), 0)
+        warm_in = tile([P, 1], F32, "warm_in")
+        warm_out = tile([P, 1], F32, "warm_out")
+        nc.gpsimd.memset(warm_in[:], 0.0)
+        nc.scalar.activation(warm_out[:], warm_in[:], ACT.Sigmoid)
         kidx_l = load_list(kidx, "kidx_l")
         nc.sync.dma_start(
             d_bytes[:].bitcast(I32),
             d_scales[0].bitcast(I32).rearrange("q (a n) -> q a n", a=1).to_broadcast([16, 8, G // 4]),
         )
-        d_tab = tile([P, G], U32, "d_tab")
-        nc.sync.dma_start(d_tab[:].bitcast(I32), d_words[0].rearrange("p n t -> p (n t)").bitcast(I32))
-        x_tab = tile([P, T], U32, "x_tab")
-        nc.sync.dma_start(x_tab[:].bitcast(I32), x_words[0].rearrange("p n t -> p (n t)").bitcast(I32))
         offs_l = load_list(offs, "offs_l")
         for q in range(4):
-            nc.scalar.dma_start(x_bytes[32 * q : 32 * q + 4, :].bitcast(I32), x_scales[0, 4 * q : 4 * q + 4, :].bitcast(I32))
+            nc.sync.dma_start(
+                x_bytes[32 * q : 32 * q + 32, :].bitcast(I32),
+                x_scales[0, 4 * q : 4 * q + 4, :].bitcast(I32).rearrange("(a i) n -> a i n", a=1).to_broadcast([8, 4, T // 4]),
+            )
+        d_tab = tile([P, G], U32, "d_tab")
+        nc.sync.dma_start(d_tab[:].bitcast(I32), d_words[0].rearrange("p n t -> p (n t)").bitcast(I32))
         n1_l = load_list(n1, "n1_l")
         n3_l = load_list(n3, "n3_l")
+        x_tab = tile([P, T], U32, "x_tab")
+        nc.sync.dma_start(x_tab[:].bitcast(I32), x_words[0].rearrange("p n t -> p (n t)").bitcast(I32))
         n2_l = load_list(n2, "n2_l")
         ga_t = tile([P, PACK], F32, "ga_t")
-        nc.sync.dma_start(ga_t[:], ga.rearrange("(p t) o -> p (t o)", t=PACK))
+        nc.gpsimd.dma_start(ga_t[:], ga.rearrange("(p t) o -> p (t o)", t=PACK))
         gb_t = tile([P, PACK], F32, "gb_t")
-        nc.sync.dma_start(gb_t[:], gb.rearrange("(p t) o -> p (t o)", t=PACK))
+        nc.gpsimd.dma_start(gb_t[:], gb.rearrange("(p t) o -> p (t o)", t=PACK))
         n5_l = load_list(n5, "n5_l")
         n4_l = load_list(n4, "n4_l")
 
@@ -74,6 +80,8 @@ def tile_picked_simkgpairwindfold_none_po_kernel(
         key_scale = tile([P, H], U8, "key_scale")
         for i in range(4):
             nc.scalar.dma_start(key_scale[i:P:32, :].bitcast(I32), key_bytes_dealt[8 * i : P : 32, :].bitcast(I32))
+        tok_scale = tile([P, S], U8, "tok_scale")
+        nc.vector.tensor_copy(tok_scale[:], x_bytes[:].indirect(offs_l[:]))
         key_words = tile([P, H], U32, "key_words")
         nc.vector.tensor_copy(key_words[:], d_tab[:].indirect(kidx_l[:]))
         key_codes = tile([P, H], U32, "key_codes")
@@ -81,88 +89,114 @@ def tile_picked_simkgpairwindfold_none_po_kernel(
             key_codes[:].bitcast(I32).rearrange("p (t m) -> p m t", t=PACK),
             key_words[:].bitcast(I32).rearrange("p (m t) -> p m t", t=PACK),
         )
-        tok_scale = tile([P, S], U8, "tok_scale")
-        nc.vector.tensor_copy(tok_scale[:], x_bytes[:].indirect(offs_l[:]))
         tok_codes = tile([P, S], U32, "tok_codes")
-        nc.vector.tensor_copy(tok_codes[:], x_tab[:].indirect(offs_l[:]))
+        for h in range(2):
+            nc.vector.tensor_copy(tok_codes[:, HALF * h : HALF * (h + 1)], x_tab[:].indirect(entries(offs_l, HALF * h, HALF)))
 
-        s_bank = [psum.tile([P, S], F32, name="s_bank%d" % t) for t in range(PACK)]
-        for t in range(PACK):
-            cols = slice(P * t, P * (t + 1))
+        s_bank = dict()
+
+        def first_product(t, first, count, bank):
+            keys = slice(P * t, P * (t + 1))
+            s_bank.setdefault((t, first), psum.tile([P, count], F32, name="s_bank%d" % bank, tag="bank%d" % bank))
             nc.tensor.matmul_mx(
-                out=s_bank[t][:],
-                lhsT=key_codes[:, cols].bitcast(FP8X4),
-                lhsT_scale=key_scale[:, cols],
-                rhs=tok_codes[:].bitcast(FP8X4),
-                rhs_scale=tok_scale[:],
+                out=s_bank[(t, first)][:],
+                lhsT=key_codes[:, keys].bitcast(FP8X4),
+                lhsT_scale=key_scale[:, keys],
+                rhs=tok_codes[:, first : first + count].bitcast(FP8X4),
+                rhs_scale=tok_scale[:, first : first + count],
                 start=True,
                 stop=True,
             )
 
+        first_product(0, 0, HALF, 0)
+        first_product(1, 0, HALF, 1)
+        first_product(0, HALF, HALF, 2)
+        first_product(1, HALF, HALF, 3)
+        first_product(2, 0, S, 4)
+        first_product(3, 0, S, 5)
+
         s = [tile([P, S], F32, "s%d" % t) for t in range(PACK)]
         mb = [tile([P, W], F32, "mb%d" % t) for t in range(PACK)]
+        e = [tile([P, S], F32, "e%d" % t) for t in range(PACK)]
+        f = [tile([P, S], F32, "f%d" % t) for t in range(PACK)]
+        s_gb = tile([P, PACK, S], F32, "s_gb")
         low = tile([P, PACK, S], F32, "low")
-        z2 = [tile([P, PACK, HALF], F32, "z2_%d" % h) for h in range(2)]
+        at2 = [tile([P, PACK, HALF], F32, "at2_%d" % h) for h in range(2)]
+        at3 = [tile([P, PACK, HALF], F32, "at3_%d" % h) for h in range(2)]
+        diff = [tile([P, PACK, HALF], F32, "diff%d" % h) for h in range(2)]
+        pieces = ((0, 352), (352, 352), (704, 320))
 
-        def evac_s(t, on_vector):
+        def evac_s(t, first, count, on_vector):
             if on_vector:
-                nc.vector.tensor_scalar(s[t][:], s_bank[t][:], SIXTEENTH, None, ALU.mult)
+                nc.vector.tensor_scalar(s[t][:, first : first + count], s_bank[(t, first)][:], SIXTEENTH, None, ALU.mult)
             else:
-                nc.scalar.activation(s[t][:], s_bank[t][:], ACT.Copy, scale=SIXTEENTH)
+                nc.scalar.activation(s[t][:, first : first + count], s_bank[(t, first)][:], ACT.Copy, scale=SIXTEENTH)
 
-        def members(t):
-            for first, count in ((0, 352), (352, 352), (704, 320)):
-                nc.scalar.activation(mb[t][:, first : first + count], s[t][:].indirect(entries(n1_l, first, count)), ACT.Copy)
+        def scaled_s(t):
+            nc.gpsimd.tensor_scalar(s_gb[:, t, :], s[t][:], gb_t[:, t : t + 1], 0.0, ALU.mult, ALU.add)
 
-        def fold(t):
-            a = mb[t][:, 0:W:2]
-            b = mb[t][:, 1:W:2]
-            e = tile([P, S], F32, "e%d" % t)
-            nc.vector.tensor_tensor(e[:], a, s[t][:], ALU.subtract)
-            f = tile([P, S], F32, "f%d" % t)
-            nc.vector.scalar_tensor_tensor(f[:], e[:], 0.0, b, ALU.min, ALU.add)
-            nc.vector.tensor_tensor(low[:, t, :], f[:], a, ALU.min)
+        def members(t, which, on_vector):
+            for first, count in which:
+                looked = s[t][:].indirect(entries(n1_l, first, count))
+                if on_vector:
+                    nc.vector.tensor_copy(mb[t][:, first : first + count], looked)
+                else:
+                    nc.scalar.activation(mb[t][:, first : first + count], looked, ACT.Copy)
 
-        def weigh(t, h, diff):
-            nc.vector.scalar_tensor_tensor(
-                z2[h][:, t, :], diff[:], gb_t[:, t : t + 1], s[t][:, HALF * h : HALF * (h + 1)], ALU.mult, ALU.mult
+        def step_e(t):
+            nc.vector.tensor_tensor(e[t][:], mb[t][:, 0:W:2], s[t][:], ALU.subtract)
+
+        def step_f(t):
+            nc.vector.scalar_tensor_tensor(f[t][:], e[t][:], 0.0, mb[t][:, 1:W:2], ALU.min, ALU.add)
+
+        def step_g(t):
+            nc.vector.tensor_tensor(low[:, t, :], f[t][:], mb[t][:, 0:W:2], ALU.min)
+
+        def fetch(dst, lst, t, h):
+            nc.scalar.activation(dst[h][:, t, :], s[t][:].indirect(entries(lst, HALF * h, HALF)), ACT.Copy)
+
+        def fetch_minus(t, h):
+            nc.vector.tensor_tensor(
+                diff[h][:, t, :], s[t][:].indirect(entries(n2_l, HALF * h, HALF)), at3[h][:, t, :], ALU.subtract
             )
 
-        def diff_on_vector(t, h):
-            at3 = tile([P, HALF], F32, "at3_%d_%d" % (t, h))
-            nc.vector.tensor_copy(at3[:], s[t][:].indirect(entries(n3_l, HALF * h, HALF)))
-            diff = tile([P, HALF], F32, "diff_%d_%d" % (t, h))
-            nc.vector.tensor_tensor(diff[:], s[t][:].indirect(entries(n2_l, HALF * h, HALF)), at3[:], ALU.subtract)
-            weigh(t, h, diff)
+        def minus(t0, t1, h):
+            nc.vector.tensor_tensor(diff[h][:, t0:t1, :], at2[h][:, t0:t1, :], at3[h][:, t0:t1, :], ALU.subtract)
 
-        def fetch_on_scalar(t, h):
-            at3 = tile([P, HALF], F32, "at3_%d_%d" % (t, h))
-            nc.scalar.activation(at3[:], s[t][:].indirect(entries(n3_l, HALF * h, HALF)), ACT.Copy)
-            at2 = tile([P, HALF], F32, "at2_%d_%d" % (t, h))
-            nc.scalar.activation(at2[:], s[t][:].indirect(entries(n2_l, HALF * h, HALF)), ACT.Copy)
-            return at2, at3
-
-        def diff_of(t, h, pair):
-            diff = tile([P, HALF], F32, "diff_%d_%d" % (t, h))
-            nc.vector.tensor_tensor(diff[:], pair[0][:], pair[1][:], ALU.subtract)
-            weigh(t, h, diff)
-
-        evac_s(0, False)
-        evac_s(1, True)
-        evac_s(2, False)
-        evac_s(3, True)
-        members(0)
-        diff_on_vector(0, 0)
-        diff_on_vector(1, 0)
-        members(1)
-        fold(0)
-        members(2)
-        fold(1)
-        members(3)
-        fold(2)
-        fold(3)
-        pairs0 = [fetch_on_scalar(t, 0) for t in (2, 3)]
-        pairs1 = [fetch_on_scalar(t, 1) for t in range(PACK)]
+        evac_s(0, 0, HALF, False)
+        evac_s(1, 0, HALF, True)
+        evac_s(0, HALF, HALF, False)
+        evac_s(1, HALF, HALF, True)
+        scaled_s(0)
+        scaled_s(1)
+        members(0, pieces[:1], False)
+        evac_s(2, 0, S, False)
+        members(0, pieces[1:], False)
+        members(1, pieces[:1], True)
+        evac_s(3, 0, S, True)
+        members(1, pieces[1:], True)
+        scaled_s(2)
+        scaled_s(3)
+        members(2, pieces, False)
+        step_e(0)
+        step_e(1)
+        step_f(0)
+        step_f(1)
+        step_g(0)
+        step_e(2)
+        step_g(1)
+        members(3, pieces, False)
+        step_f(2)
+        step_e(3)
+        step_g(2)
+        step_f(3)
+        step_g(3)
+        for h in range(2):
+            for t in range(PACK):
+                fetch(at3, n3_l, t, h)
+                if (t, h) != (0, 0):
+                    fetch(at2, n2_l, t, h)
+        fetch_minus(0, 0)
 
         z_bf = tile([P, S * PACK], BF16, "z_bf")
         nc.vector.tensor_tensor(
@@ -171,22 +205,28 @@ def tile_picked_simkgpairwindfold_none_po_kernel(
             ga_t[:].rearrange("p (a t b) -> p a t b", a=1, b=1).to_broadcast([P, P, PACK, PACK]),
             ALU.mult,
         )
+        minus(1, 2, 0)
         z_codes = tile([P, S], U32, "z_codes")
         z_scale = tile([P, S], U8, "z_scale")
         nc.vector.quantize_mx(out=z_codes[:].bitcast(FP8X4), scales=z_scale[:], in_=z_bf[:])
 
-        cm_bank = [psum.tile([P, S], F32, name="cm_bank%d" % t) for t in range(PACK)]
+        cm_bank = [psum.tile([P, S], F32, name="cm_bank%d" % t, tag="bank%d" % t) for t in range(PACK)]
         res = [tile([P, S], F32, "res%d" % t) for t in range(PACK)]
+        y_bf = [tile([P, HALF * PACK], BF16, "y_bf%d" % h) for h in range(2)]
+
+        def weigh(h):
+            nc.vector.tensor_tensor(
+                y_bf[h][:].rearrange("p (c i t) -> p c t i", i=4, t=PACK),
+                diff[h][:].rearrange("p t (c i) -> p c t i", i=4),
+                s_gb[:, :, HALF * h : HALF * (h + 1)].rearrange("p t (c i) -> p c t i", i=4),
+                ALU.mult,
+            )
 
         def second_product(h):
             cols = slice(HALF * h, HALF * (h + 1))
-            y_bf = tile([P, HALF * PACK], BF16, "y_bf%d" % h)
-            nc.vector.tensor_copy(
-                y_bf[:].rearrange("p (c i t) -> p c t i", i=4, t=PACK), z2[h][:].rearrange("p t (c i) -> p c t i", i=4)
-            )
             y_codes = tile([P, HALF], U32, "y_codes%d" % h)
             y_scale = tile([P, HALF], U8, "y_scale%d" % h)
-            nc.vector.quantize_mx(out=y_codes[:].bitcast(FP8X4), scales=y_scale[:], in_=y_bf[:])
+            nc.vector.quantize_mx(out=y_codes[:].bitcast(FP8X4), scales=y_scale[:], in_=y_bf[h][:])
             for t in range(PACK):
                 rows = slice(P * t, P * (t + 1))
                 nc.tensor.matmul_mx(
@@ -206,13 +246,15 @@ def tile_picked_simkgpairwindfold_none_po_kernel(
             else:
                 nc.scalar.activation(res[t][:, cols], cm_bank[t][:, cols], ACT.Copy, scale=SIXTEENTH)
 
-        diff_of(2, 0, pairs0[0])
-        diff_of(3, 0, pairs0[1])
+        minus(2, 4, 0)
+        weigh(0)
+        minus(0, 2, 1)
         second_product(0)
-        for t in range(PACK):
-            diff_of(t, 1, pairs1[t])
+        minus(2, 3, 1)
+        minus(3, 4, 1)
         for t in range(PACK):
             evac_cm(t, 0, False)
+        weigh(1)
         second_product(1)
 
         gate = [tile([P, U], F32, "gate%d" % t) for t in range(PACK)]
@@ -247,43 +289,50 @@ def tile_picked_simkgpairwindfold_none_po_kernel(
             else:
                 nc.scalar.copy(rounded[:, t, :], res[t][:])
 
-        evac_cm(1, 1, True)
         evac_cm(0, 1, False)
+        evac_cm(1, 1, True)
         evac_cm(2, 1, True)
-        sig(1)
-        fetch_a(2, True)
         sig(0)
-        fetch_mul(1)
-        fetch_a(0, False)
+        fetch_a(1, True)
+        sig(1)
+        fetch_mul(0)
         evac_cm(3, 1, False)
-        put_mul(0)
-        store(0)
-        sig(3)
         sig(2)
-        put(1)
+        fetch_mul(2)
+        sig(3)
+        put_mul(1)
         store(1)
-        fetch_mul(3)
-        put_mul(2)
+        put(0)
+        store(0)
+        fetch_a(3, True)
+        put(2)
         store(2)
-        put(3)
+        put_mul(3)
         store(3)
-        for t in (0, 1, 2, 3):
-            rnd(t, True)
+        rnd(0, False)
+        rnd(1, False)
+        rnd(2, True)
+        rnd(3, True)
 
-        woven = tile([P, S * PACK], BF16, "woven")
+        woven = [tile([P, HALF * PACK], BF16, "woven%d" % h) for h in range(2)]
         cut = 160
-        nc.scalar.copy(
-            woven[:, : cut * PACK].rearrange("p (c i t) -> p c t i", i=4, t=PACK),
-            rounded[:, :, :cut].rearrange("p t (c i) -> p c t i", i=4),
-        )
-        nc.vector.tensor_copy(
-            woven[:, cut * PACK :].rearrange("p (c i t) -> p c t i", i=4, t=PACK),
-            rounded[:, :, cut:].rearrange("p t (c i) -> p c t i", i=4),
-        )
-        out_codes = tile([P, S], U32, "out_codes")
+
+        def weave(copy, h, c0, c1):
+            copy(
+                woven[h][:, c0 * PACK : c1 * PACK].rearrange("p (c i t) -> p c t i", i=4, t=PACK),
+                rounded[:, :, HALF * h + c0 : HALF * h + c1].rearrange("p t (c i) -> p c t i", i=4),
+            )
+
+        weave(nc.vector.tensor_copy, 0, 0, HALF)
+        weave(nc.scalar.copy, 1, 0, cut)
+        weave(nc.vector.tensor_copy, 1, cut, HALF)
+        out_codes = [tile([P, HALF], U32, "out_codes%d" % h) for h in range(2)]
         out_scale = tile([P, S], U8, "out_scale")
-        nc.vector.quantize_mx(out=out_codes[:].bitcast(FP8X4), scales=out_scale[:], in_=woven[:])
-        nc.sync.dma_start(out_1[0].rearrange("p n t -> p (n t)").bitcast(I32), out_codes[:].bitcast(I32))
+        out_words = out_1[0].rearrange("p n t -> p (n t)").bitcast(I32)
+        for h in range(2):
+            cols = slice(HALF * h, HALF * (h + 1))
+            nc.vector.quantize_mx(out=out_codes[h][:].bitcast(FP8X4), scales=out_scale[:, cols], in_=woven[h][:])
+            nc.sync.dma_start(out_words[:, cols], out_codes[h][:].bitcast(I32))
         for q in range(4):
             queue = nc.scalar if q % 2 == 0 else nc.sync
             queue.dma_start(out_2[0, 4 * q : 4 * q + 4, :].bitcast(I32), out_scale[32 * q : 32 * q + 4, :].bitcast(I32))

from contextlib import ExitStack

import concourse.mybir as mybir

K, T, S, G, H, W, U = 512, 2048, 512, 2048, 512, 1024, 256
FLOPS = 2 * K * H * S + 2 * H * S * S

F32 = mybir.dt.float32
BF16 = mybir.dt.bfloat16
U32 = mybir.dt.uint32
I32 = mybir.dt.int32
U16 = mybir.dt.uint16
U8 = mybir.dt.uint8
FP8X4 = mybir.dt.float8_e4m3fn_x4
ALU = mybir.AluOpType
ACT = mybir.ActivationFunctionType

P = 128
PACK = 4
HALF = S // 2
SIXTEENTH = 0.0625


def tile_picked_simkgpairwindfold_none_po_kernel(
    tc, x_words, x_scales, d_words, d_scales, ga, gb, offs, kidx, n1, n2, n3, n4, n5, out_0, out_1, out_2
):
    nc = tc.nc
    with ExitStack() as ctx:
        keep = ctx.enter_context(tc.tile_pool(name="keep", bufs=1))
        psum = ctx.enter_context(tc.psum_pool(name="psum", bufs=1))

        def tile(shape, dtype, name):
            return keep.tile(shape, dtype, name=name, align_bytes=64)

        def load_list(src, name):
            lst = keep.tile(list(src.shape), U16, name=name)
            nc.sync.dma_start(lst[:], src)
            return lst

        def entries(lst, first, count):
            return lst[:, first // 16 : (first + count) // 16]

        d_bytes = tile([P, G], U8, "d_bytes")
        x_bytes = tile([P, T], U8, "x_bytes")
        warm_in = tile([P, 1], F32, "warm_in")
        warm_out = tile([P, 1], F32, "warm_out")
        nc.gpsimd.memset(warm_in[:], 0.0)
        nc.scalar.activation(warm_out[:], warm_in[:], ACT.Sigmoid)
        kidx_l = load_list(kidx, "kidx_l")
        nc.sync.dma_start(
            d_bytes[:].bitcast(I32),
            d_scales[0].bitcast(I32).rearrange("q (a n) -> q a n", a=1).to_broadcast([16, 8, G // 4]),
        )
        offs_l = load_list(offs, "offs_l")
        for q in range(4):
            nc.sync.dma_start(
                x_bytes[32 * q : 32 * q + 32, :].bitcast(I32),
                x_scales[0, 4 * q : 4 * q + 4, :].bitcast(I32).rearrange("(a i) n -> a i n", a=1).to_broadcast([8, 4, T // 4]),
            )
        d_tab = tile([P, G], U32, "d_tab")
        nc.sync.dma_start(d_tab[:].bitcast(I32), d_words[0].rearrange("p n t -> p (n t)").bitcast(I32))
        n1_l = load_list(n1, "n1_l")
        n3_l = load_list(n3, "n3_l")
        x_tab = tile([P, T], U32, "x_tab")
        nc.sync.dma_start(x_tab[:].bitcast(I32), x_words[0].rearrange("p n t -> p (n t)").bitcast(I32))
        n2_l = load_list(n2, "n2_l")
        ga_t = tile([P, PACK], F32, "ga_t")
        nc.gpsimd.dma_start(ga_t[:], ga.rearrange("(p t) o -> p (t o)", t=PACK))
        gb_t = tile([P, PACK], F32, "gb_t")
        nc.gpsimd.dma_start(gb_t[:], gb.rearrange("(p t) o -> p (t o)", t=PACK))
        n5_l = load_list(n5, "n5_l")
        n4_l = load_list(n4, "n4_l")

        key_bytes = tile([P, H], U8, "key_bytes")
        nc.vector.tensor_copy(key_bytes[:], d_bytes[:].indirect(kidx_l[:]))
        key_bytes_dealt = tile([P, H], U8, "key_bytes_dealt")
        nc.vector.tensor_copy(
            key_bytes_dealt[:].rearrange("p (t m) -> p m t", t=PACK), key_bytes[:].rearrange("p (m t) -> p m t", t=PACK)
        )
        key_scale = tile([P, H], U8, "key_scale")
        for i in range(4):
            nc.scalar.dma_start(key_scale[i:P:32, :].bitcast(I32), key_bytes_dealt[8 * i : P : 32, :].bitcast(I32))
        tok_scale = tile([P, S], U8, "tok_scale")
        nc.vector.tensor_copy(tok_scale[:], x_bytes[:].indirect(offs_l[:]))
        key_words = tile([P, H], U32, "key_words")
        nc.vector.tensor_copy(key_words[:], d_tab[:].indirect(kidx_l[:]))
        key_codes = tile([P, H], U32, "key_codes")
        nc.vector.tensor_copy(
            key_codes[:].bitcast(I32).rearrange("p (t m) -> p m t", t=PACK),
            key_words[:].bitcast(I32).rearrange("p (m t) -> p m t", t=PACK),
        )
        tok_codes = tile([P, S], U32, "tok_codes")
        for h in range(2):
            nc.vector.tensor_copy(tok_codes[:, HALF * h : HALF * (h + 1)], x_tab[:].indirect(entries(offs_l, HALF * h, HALF)))

        s_bank = dict()

        def first_product(t, first, count, bank):
            keys = slice(P * t, P * (t + 1))
            s_bank.setdefault((t, first), psum.tile([P, count], F32, name="s_bank%d" % bank, tag="bank%d" % bank))
            nc.tensor.matmul_mx(
                out=s_bank[(t, first)][:],
                lhsT=key_codes[:, keys].bitcast(FP8X4),
                lhsT_scale=key_scale[:, keys],
                rhs=tok_codes[:, first : first + count].bitcast(FP8X4),
                rhs_scale=tok_scale[:, first : first + count],
                start=True,
                stop=True,
            )

        first_product(0, 0, HALF, 0)
        first_product(1, 0, HALF, 1)
        first_product(0, HALF, HALF, 2)
        first_product(1, HALF, HALF, 3)
        first_product(2, 0, S, 4)
        first_product(3, 0, S, 5)

        s = [tile([P, S], F32, "s%d" % t) for t in range(PACK)]
        mb = [tile([P, W], F32, "mb%d" % t) for t in range(PACK)]
        e = [tile([P, S], F32, "e%d" % t) for t in range(PACK)]
        f = [tile([P, S], F32, "f%d" % t) for t in range(PACK)]
        s_gb = tile([P, PACK, S], F32, "s_gb")
        low = tile([P, PACK, S], F32, "low")
        at2 = [tile([P, PACK, HALF], F32, "at2_%d" % h) for h in range(2)]
        at3 = [tile([P, PACK, HALF], F32, "at3_%d" % h) for h in range(2)]
        diff = [tile([P, PACK, HALF], F32, "diff%d" % h) for h in range(2)]
        pieces = ((0, 352), (352, 352), (704, 320))

        def evac_s(t, first, count, on_vector):
            if on_vector:
                nc.vector.tensor_scalar(s[t][:, first : first + count], s_bank[(t, first)][:], SIXTEENTH, None, ALU.mult)
            else:
                nc.scalar.activation(s[t][:, first : first + count], s_bank[(t, first)][:], ACT.Copy, scale=SIXTEENTH)

        def scaled_s(t):
            nc.gpsimd.tensor_scalar(s_gb[:, t, :], s[t][:], gb_t[:, t : t + 1], 0.0, ALU.mult, ALU.add)

        def members(t, which, on_vector):
            for first, count in which:
                looked = s[t][:].indirect(entries(n1_l, first, count))
                if on_vector:
                    nc.vector.tensor_copy(mb[t][:, first : first + count], looked)
                else:
                    nc.scalar.activation(mb[t][:, first : first + count], looked, ACT.Copy)

        def step_e(t):
            nc.vector.tensor_tensor(e[t][:], mb[t][:, 0:W:2], s[t][:], ALU.subtract)

        def step_f(t):
            nc.vector.scalar_tensor_tensor(f[t][:], e[t][:], 0.0, mb[t][:, 1:W:2], ALU.min, ALU.add)

        def step_g(t):
            nc.vector.tensor_tensor(low[:, t, :], f[t][:], mb[t][:, 0:W:2], ALU.min)

        def fetch(dst, lst, t, h):
            nc.scalar.activation(dst[h][:, t, :], s[t][:].indirect(entries(lst, HALF * h, HALF)), ACT.Copy)

        def fetch_minus(t, h):
            nc.vector.tensor_tensor(
                diff[h][:, t, :], s[t][:].indirect(entries(n2_l, HALF * h, HALF)), at3[h][:, t, :], ALU.subtract
            )

        def minus(t0, t1, h):
            nc.vector.tensor_tensor(diff[h][:, t0:t1, :], at2[h][:, t0:t1, :], at3[h][:, t0:t1, :], ALU.subtract)

        evac_s(0, 0, HALF, False)
        evac_s(1, 0, HALF, True)
        evac_s(0, HALF, HALF, False)
        evac_s(1, HALF, HALF, True)
        scaled_s(0)
        scaled_s(1)
        members(0, pieces[:1], False)
        evac_s(2, 0, S, False)
        members(0, pieces[1:], False)
        members(1, pieces[:1], True)
        evac_s(3, 0, S, True)
        members(1, pieces[1:], True)
        scaled_s(2)
        scaled_s(3)
        members(2, pieces, False)
        step_e(0)
        step_e(1)
        step_f(0)
        step_f(1)
        step_g(0)
        step_e(2)
        step_g(1)
        members(3, pieces, False)
        step_f(2)
        step_e(3)
        step_g(2)
        step_f(3)
        step_g(3)
        for h in range(2):
            for t in range(PACK):
                fetch(at3, n3_l, t, h)
                if (t, h) != (0, 0):
                    fetch(at2, n2_l, t, h)
        fetch_minus(0, 0)

        z_bf = tile([P, S * PACK], BF16, "z_bf")
        nc.vector.tensor_tensor(
            z_bf[:].rearrange("p (r m t) -> p m t r", r=PACK, t=PACK),
            low[:].rearrange("p t (m r) -> p m t r", r=PACK),
            ga_t[:].rearrange("p (a t b) -> p a t b", a=1, b=1).to_broadcast([P, P, PACK, PACK]),
            ALU.mult,
        )
        minus(1, 2, 0)
        z_codes = tile([P, S], U32, "z_codes")
        z_scale = tile([P, S], U8, "z_scale")
        nc.vector.quantize_mx(out=z_codes[:].bitcast(FP8X4), scales=z_scale[:], in_=z_bf[:])

        cm_bank = [psum.tile([P, S], F32, name="cm_bank%d" % t, tag="bank%d" % t) for t in range(PACK)]
        res = [tile([P, S], F32, "res%d" % t) for t in range(PACK)]
        y_bf = [tile([P, HALF * PACK], BF16, "y_bf%d" % h) for h in range(2)]

        def weigh(h):
            nc.vector.tensor_tensor(
                y_bf[h][:].rearrange("p (c i t) -> p c t i", i=4, t=PACK),
                diff[h][:].rearrange("p t (c i) -> p c t i", i=4),
                s_gb[:, :, HALF * h : HALF * (h + 1)].rearrange("p t (c i) -> p c t i", i=4),
                ALU.mult,
            )

        def second_product(h):
            cols = slice(HALF * h, HALF * (h + 1))
            y_codes = tile([P, HALF], U32, "y_codes%d" % h)
            y_scale = tile([P, HALF], U8, "y_scale%d" % h)
            nc.vector.quantize_mx(out=y_codes[:].bitcast(FP8X4), scales=y_scale[:], in_=y_bf[h][:])
            for t in range(PACK):
                rows = slice(P * t, P * (t + 1))
                nc.tensor.matmul_mx(
                    out=cm_bank[t][:, cols],
                    lhsT=z_codes[:, rows].bitcast(FP8X4),
                    lhsT_scale=z_scale[:, rows],
                    rhs=y_codes[:].bitcast(FP8X4),
                    rhs_scale=y_scale[:],
                    start=True,
                    stop=True,
                )

        def evac_cm(t, h, on_vector):
            cols = slice(HALF * h, HALF * (h + 1))
            if on_vector:
                nc.vector.tensor_scalar(res[t][:, cols], cm_bank[t][:, cols], SIXTEENTH, None, ALU.mult)
            else:
                nc.scalar.activation(res[t][:, cols], cm_bank[t][:, cols], ACT.Copy, scale=SIXTEENTH)

        minus(2, 4, 0)
        weigh(0)
        minus(0, 2, 1)
        second_product(0)
        minus(2, 3, 1)
        minus(3, 4, 1)
        for t in range(PACK):
            evac_cm(t, 0, False)
        weigh(1)
        second_product(1)

        gate = [tile([P, U], F32, "gate%d" % t) for t in range(PACK)]
        part = [tile([P, U], F32, "part%d" % t) for t in range(PACK)]
        rounded = tile([P, PACK, S], BF16, "rounded")
        out_rows = out_0.rearrange("(p t) j -> p t j", t=PACK)

        def sig(t):
            nc.scalar.activation(gate[t][:], res[t][:].indirect(n5_l[:]), ACT.Sigmoid)

        def fetch_a(t, on_vector):
            if on_vector:
                nc.vector.tensor_copy(part[t][:], res[t][:].indirect(n4_l[:]))
            else:
                nc.scalar.activation(part[t][:], res[t][:].indirect(n4_l[:]), ACT.Copy)

        def fetch_mul(t):
            nc.vector.tensor_tensor(part[t][:], res[t][:].indirect(n4_l[:]), gate[t][:], ALU.mult)

        def put_mul(t):
            nc.vector.tensor_tensor(res[t][:].indirect(n5_l[:]), part[t][:], gate[t][:], ALU.mult)

        def put(t):
            nc.scalar.activation(res[t][:].indirect(n5_l[:]), part[t][:], ACT.Copy)

        def store(t):
            nc.sync.dma_start(out_rows[:, t, :], res[t][:])

        def rnd(t, on_vector):
            if on_vector:
                nc.vector.tensor_copy(rounded[:, t, :], res[t][:])
            else:
                nc.scalar.copy(rounded[:, t, :], res[t][:])

        evac_cm(0, 1, False)
        evac_cm(1, 1, True)
        evac_cm(2, 1, True)
        sig(0)
        fetch_a(1, True)
        sig(1)
        fetch_mul(0)
        evac_cm(3, 1, False)
        sig(2)
        fetch_mul(2)
        sig(3)
        put_mul(1)
        store(1)
        put(0)
        store(0)
        fetch_a(3, True)
        put(2)
        store(2)
        put_mul(3)
        store(3)
        rnd(0, False)
        rnd(1, False)
        rnd(2, True)
        rnd(3, True)

        woven = [tile([P, HALF * PACK], BF16, "woven%d" % h) for h in range(2)]
        cut = 160

        def weave(copy, h, c0, c1):
            copy(
                woven[h][:, c0 * PACK : c1 * PACK].rearrange("p (c i t) -> p c t i", i=4, t=PACK),
                rounded[:, :, HALF * h + c0 : HALF * h + c1].rearrange("p t (c i) -> p c t i", i=4),
            )

        weave(nc.vector.tensor_copy, 0, 0, HALF)
        weave(nc.scalar.copy, 1, 0, cut)
        weave(nc.vector.tensor_copy, 1, cut, HALF)
        out_codes = [tile([P, HALF], U32, "out_codes%d" % h) for h in range(2)]
        out_scale = tile([P, S], U8, "out_scale")
        out_words = out_1[0].rearrange("p n t -> p (n t)").bitcast(I32)
        for h in range(2):
            cols = slice(HALF * h, HALF * (h + 1))
            nc.vector.quantize_mx(out=out_codes[h][:].bitcast(FP8X4), scales=out_scale[:, cols], in_=woven[h][:])
            nc.sync.dma_start(out_words[:, cols], out_codes[h][:].bitcast(I32))
        for q in range(4):
            queue = nc.scalar if q % 2 == 0 else nc.sync
            queue.dma_start(out_2[0, 4 * q : 4 * q + 4, :].bitcast(I32), out_scale[32 * q : 32 * q + 4, :].bitcast(I32))
